import numpy as np
import ml_dtypes


def mxq(x, axis, fmt="e4m3"):
    dtype, down = {"e4m3": (ml_dtypes.float8_e4m3fn, 7), "e5m2": (ml_dtypes.float8_e5m2, 14)}[fmt]
    v = np.moveaxis(np.asarray(x, np.float32).astype(ml_dtypes.bfloat16).astype(np.float64), axis, -1)
    blocks = v.reshape(v.shape[:-1] + (-1, 32))
    amax = np.abs(blocks).max(-1, keepdims=True)
    byte = np.maximum(np.where(amax > 0, np.frexp(amax)[1] - 1 + 127, 0) - down, 1)
    scale = np.exp2(byte - 127.0)
    codes = (blocks / scale).astype(np.float32).astype(dtype).astype(np.float64)
    return np.moveaxis((codes * scale).reshape(v.shape), -1, axis)


WIDE = False


def mx_kscale(k):
    if not WIDE:
        return np.ones(k)
    levels = np.array([10, -10, 5, -5, 0])
    if k % 512:
        return np.exp2(np.random.permutation(np.resize(levels, k // 32))).repeat(32)
    a = np.empty((k // 512, 16))
    for p in range(k // 512):
        a[p, :8] = np.random.permutation(np.resize(levels, 8))
        for g in range(8):
            far = levels[np.abs(levels - a[p, g]) >= 10]
            a[p, g + 8] = far[np.random.randint(len(far))]
    return np.exp2(a.ravel()).repeat(32)


def f64(x):
    return np.asarray(x).astype(np.float64)


def striped(idx):
    return np.tile(np.asarray(idx).reshape(-1, 16).T, (8, 1)).astype(np.uint16)


def unstriped(offs):
    return offs[:16].T.reshape(-1).astype(np.int64)


E2M1 = np.array([0.0, 0.5, 1.0, 1.5, 2.0, 3.0, 4.0, 6.0, -0.0, -0.5, -1.0, -1.5, -2.0, -3.0, -4.0, -6.0])


def pack_weight(w, fmt):
    k, n = w.shape
    w = f64(np.asarray(w, np.float32).astype(ml_dtypes.bfloat16)).reshape(k // 32, 32, n)
    amax = np.abs(w).max(1)
    if fmt == "e4m3":
        byte = np.frexp(amax)[1] - 1 + 127 - 7
    else:
        mant, ex = np.frexp(amax / 6.0)
        byte = np.where(mant > 0.5, ex, ex - 1) + 127
    byte = np.clip(np.where(amax > 0, byte, 1), 1, 254)
    scaled = (w * np.exp2(127.0 - byte)[:, None, :]).reshape(k, n).astype(np.float32)
    by_word = np.ascontiguousarray(scaled.reshape(k // 512, 128, 4, n).transpose(0, 1, 3, 2))
    if fmt == "e4m3":
        words = by_word.astype(ml_dtypes.float8_e4m3fn).view(np.uint8)
    else:
        c = by_word.astype(ml_dtypes.float4_e2m1fn).view(np.uint8) & 0xF
        words = (c[..., 0::2] | (c[..., 1::2] << 4)).reshape(k // 512, 128, 2 * n)
    return np.ascontiguousarray(words), np.ascontiguousarray(byte.astype(np.uint8).reshape(k // 512, 16, n))


def unpack_weight(words, scales, fmt):
    g, _, n = scales.shape
    words = np.ascontiguousarray(words).reshape(g, 128, n, -1)
    if fmt == "e4m3":
        vals = words.view(ml_dtypes.float8_e4m3fn).astype(np.float64)
    else:
        nib = np.empty((g, 128, n, 4), np.uint8)
        nib[..., 0::2] = words & 0xF
        nib[..., 1::2] = words >> 4
        vals = E2M1[nib]
    vals = vals * np.repeat(np.exp2(scales.astype(np.float64) - 127.0), 8, axis=1)[..., None]
    return vals.transpose(0, 1, 3, 2).reshape(g * 512, n)


def bf(x):
    return np.asarray(x, np.float32).astype(ml_dtypes.bfloat16)


def planes(Y):
    r, m = Y.shape
    b = f64(bf(Y)).reshape(r // 32, 32, m)
    amax = np.abs(b).max(1)
    byte = np.clip(np.where(amax > 0, np.frexp(amax)[1] - 1 + 127 - 7, 1), 1, 254)
    codes = (b * np.exp2(127.0 - byte)[:, None, :]).reshape(r, m).astype(np.float32).astype(ml_dtypes.float8_e4m3fn).view(np.uint8)
    words = codes.reshape(r // 512, 128, 4, m).transpose(0, 1, 3, 2)
    return np.ascontiguousarray(words), np.ascontiguousarray(byte.astype(np.uint8).reshape(r // 512, 16, m))


D, T, I, J, U, E, Y = 512, 2048, 512, 512, 1024, 512, 1024


def setup_inputs():
    n = np.random.standard_normal
    idx = np.random.permutation(T)[:I]
    idx2 = np.random.permutation(U)[:J]
    idx3 = np.random.permutation(Y)[:I]
    fd = mx_kscale(D)
    fi = mx_kscale(I)
    ti = np.ones(T)
    ti[idx] = fi
    ti3 = np.ones(Y)
    ti3[idx3] = fi
    keysp = pack_weight(n((D, T)) / fd[:, None], "e2m1")
    return {
        "keys_words": keysp[0],
        "keys_scales": keysp[1],
        "notes": (n((D, U)) * 1.0 / np.sqrt(D) * fd[:, None]).astype(np.float32),
        "rowf": (np.random.uniform(0.02, 0.08, (I, 1)) * fi[:, None]).astype(np.float32),
        "rowf2": (np.random.uniform(0.02, 0.08, (I, 1)) * fi[:, None]).astype(np.float32),
        "vals": (n((E, T)) / ti).astype(np.float32),
        "vals2": (n((E, Y)) / ti3).astype(np.float32),
        "offs": striped(idx),
        "offs2": striped(idx2),
        "offs3": striped(idx3),
    }


def reference(keys_words, keys_scales, notes, rowf, rowf2, vals, vals2, offs, offs2, offs3):
    idx = unstriped(offs)
    idx2 = unstriped(offs2)
    idx3 = unstriped(offs3)
    keysu = unpack_weight(keys_words, keys_scales, "e2m1")
    keysidxg = keysu[:, idx]
    notesidx2q = mxq(f64(notes)[:, idx2], 0, "e4m3")
    g9 = keysidxg.T @ notesidx2q
    g0 = np.maximum(g9, 0.0)
    gr1 = g0 * f64(rowf)
    gr2 = g0 * f64(rowf2)
    vt1 = f64(vals)[:, idx].T
    vt2 = f64(vals2)[:, idx3].T
    vt1q = mxq(vt1, 0, "e4m3")
    gr1q = mxq(gr1, 0, "e4m3")
    vt2q = mxq(vt2, 0, "e4m3")
    gr2q = mxq(gr2, 0, "e4m3")
    o = vt1q.T @ gr1q + vt2q.T @ gr2q
    words, scales = planes(o)
    return o, words, scales

@@ -1,0 +1,222 @@
+from contextlib import ExitStack
+
+import concourse.mybir as mybir
+from concourse.masks import make_identity
+
+FLOPS = 2 * 512 * 512 * 512 * 3
+
+F32 = mybir.dt.float32
+BF16 = mybir.dt.bfloat16
+I32 = mybir.dt.int32
+U32 = mybir.dt.uint32
+U16 = mybir.dt.uint16
+U8 = mybir.dt.uint8
+FP8X4 = mybir.dt.float8_e4m3fn_x4
+FP4X4 = mybir.dt.float4_e2m1fn_x4
+COPY = mybir.ActivationFunctionType.Copy
+ALU = mybir.AluOpType
+
+P = 128
+PACK = 4
+N = 512
+HALF = N // 2
+CHUNK = N // PACK
+LIST_COLS = N // 16
+
+
+def tile_attend_tab_plain_twostores_pl_kernel(
+    tc, keys_words, keys_scales, notes, rowf, rowf2, vals, vals2, offs, offs2, offs3, out_0, out_1, out_2
+):
+    nc = tc.nc
+    tokens = vals.shape[1]
+
+    with ExitStack() as ctx:
+        sb = ctx.enter_context(tc.tile_pool(name="sb", bufs=1))
+        banks = ctx.enter_context(tc.psum_pool(name="banks", bufs=1))
+        turn = ctx.enter_context(tc.psum_pool(name="turn", bufs=3))
+
+        def load_list(name, src):
+            tile = sb.tile([P, LIST_COLS], U16, name=name)
+            nc.sync.dma_start(tile[:], src)
+            return tile
+
+        def load_plane(name, src, t):
+            tile = sb.tile([P, src.shape[1]], F32, name=name + str(t))
+            nc.sync.dma_start(tile[:], src.rearrange("(p t) c -> p t c", t=PACK)[:, t, :])
+            return tile
+
+        def gather(engine, out, window, offsets):
+            if engine == "scalar":
+                nc.scalar.activation(out, window.indirect(offsets), COPY)
+            else:
+                nc.vector.tensor_copy(out, window.indirect(offsets))
+
+        key_scale_pool = sb.tile([P, tokens], U8, name="key_scale_pool")
+        nc.gpsimd.memset(key_scale_pool[:].bitcast(I32), 0)
+        for q in range(4):
+            nc.gpsimd.dma_start(
+                key_scale_pool[32 * q : 32 * q + 4, :].bitcast(I32), keys_scales[0, 4 * q : 4 * q + 4, :].bitcast(I32)
+            )
+        factors = []
+        for name, src in (("factor1", rowf), ("factor2", rowf2)):
+            tile = sb.tile([P, PACK], F32, name=name)
+            nc.gpsimd.dma_start(tile[:], src.rearrange("(p t) o -> p (t o)", t=PACK))
+            factors.append(tile)
+        ident = sb.tile([P, P], F32, name="ident")
+        make_identity(nc, ident[:])
+
+        token_list = load_list("token_list", offs)
+        key_word_pool = sb.tile([P, tokens], U16, name="key_word_pool")
+        nc.sync.dma_start(key_word_pool[:].bitcast(I32), keys_words[0].bitcast(I32))
+        note_list = load_list("note_list", offs2)
+        note_planes = [load_plane("notes", notes, t) for t in range(PACK)]
+        second_list = load_list("second_list", offs3)
+        second_planes = [load_plane("second", vals2, t) for t in range(PACK)]
+        first_planes = [load_plane("first", vals, t) for t in range(PACK)]
+
+        key_words_listed = sb.tile([P, N], U16, name="key_words_listed")
+        nc.vector.tensor_copy(key_words_listed[:], key_word_pool[:].indirect(token_list[:]))
+        key_words = sb.tile([P, PACK, P], U16, name="key_words", align_bytes=64)
+        nc.vector.tensor_copy(key_words[:], key_words_listed[:].rearrange("p (m t) -> p t m", t=PACK))
+
+        notes_listed = sb.tile([P, PACK, N], BF16, name="notes_listed")
+        gather("scalar", notes_listed[:, 0, :], note_planes[0][:], note_list[:])
+        gather("vector", notes_listed[:, 1, :], note_planes[1][:], note_list[:])
+        gather("scalar", notes_listed[:, 2, :], note_planes[2][:], note_list[:])
+
+        key_scales = sb.tile([P, PACK, P], U8, name="key_scales", align_bytes=64)
+        nc.vector.tensor_copy(key_scales[:].rearrange("p t m -> p m t"), key_scale_pool[:].indirect(token_list[:]))
+
+        gather("vector", notes_listed[:, 3, 0:HALF], note_planes[3][:], note_list[:, 0 : LIST_COLS // 2])
+        gather("scalar", notes_listed[:, 3, HALF:N], note_planes[3][:], note_list[:, LIST_COLS // 2 : LIST_COLS])
+
+        note_codes = sb.tile([P, N], U32, name="note_codes", align_bytes=64)
+        note_scales = sb.tile([P, N], U8, name="note_scales", align_bytes=64)
+        notes_woven = [sb.tile([P, HALF, PACK], BF16, name="notes_woven" + str(h), align_bytes=64) for h in range(2)]
+        for h in range(2):
+            cols = slice(h * HALF, (h + 1) * HALF)
+            nc.vector.tensor_copy(notes_woven[h][:], notes_listed[:, :, cols].rearrange("p t j -> p j t"))
+        for h in range(2):
+            cols = slice(h * HALF, (h + 1) * HALF)
+            nc.vector.quantize_mx(
+                out=note_codes[:, cols].bitcast(FP8X4),
+                scales=note_scales[:, cols],
+                in_=notes_woven[h][:].rearrange("p j t -> p (j t)"),
+            )
+
+        def turn_values(name, listed):
+            words = listed[:].bitcast(F32)
+            turned = turn.tile([P, 2, P], F32, name="turned")
+            for u in range(2):
+                nc.tensor.transpose(turned[:, u, :], words[:, u : 2 * P : 2], ident[:])
+            woven = sb.tile([P, P * PACK], BF16, name=name + "_woven", align_bytes=64)
+            nc.scalar.copy(woven[:].bitcast(F32).rearrange("p (m u) -> p m u", u=2), turned[:].rearrange("p u m -> p m u"))
+            return woven
+
+        def quantize_values(name, woven):
+            codes = sb.tile([P, P], U32, name=name + "_codes", align_bytes=64)
+            scales = sb.tile([P, P], U8, name=name + "_scales", align_bytes=64)
+            nc.vector.quantize_mx(out=codes[:].bitcast(FP8X4), scales=scales[:], in_=woven[:])
+            return codes, scales
+
+        second_woven = []
+
+        def second_plane(t):
+            listed = sb.tile([P, N], BF16, name="second_listed" + str(t))
+            gather("scalar", listed[:], second_planes[t][:], second_list[:])
+            second_woven.append(turn_values("second" + str(t), listed))
+
+        second_plane(0)
+
+        tables = [sb.tile([P, N, PACK], BF16, name="table" + str(s), align_bytes=64) for s in range(2)]
+        for c in range(PACK):
+            cols = slice(c * CHUNK, (c + 1) * CHUNK)
+            raw = banks.tile([P, PACK, CHUNK], F32, name="raw", tag="bank" + str(c))
+            for t in range(PACK):
+                nc.tensor.matmul_mx(
+                    out=raw[:, t, :],
+                    lhsT=key_words[:, t, :].bitcast(FP4X4),
+                    lhsT_scale=key_scales[:, t, :],
+                    rhs=note_codes[:, cols].bitcast(FP8X4),
+                    rhs_scale=note_scales[:, cols],
+                    start=True,
+                    stop=True,
+                )
+            for s in range(2):
+                nc.vector.scalar_tensor_tensor(
+                    out=tables[s][:, cols, :],
+                    in0=raw[:].rearrange("p t j -> p j t"),
+                    scalar=0.0,
+                    in1=factors[s][:].unsqueeze(1).broadcast_to([P, CHUNK, PACK]),
+                    op0=ALU.max,
+                    op1=ALU.mult,
+                )
+            if c + 1 < PACK:
+                second_plane(c + 1)
+
+        table_codes = [sb.tile([P, N], U32, name="table_codes" + str(s), align_bytes=64) for s in range(2)]
+        table_scales = [sb.tile([P, N], U8, name="table_scales" + str(s), align_bytes=64) for s in range(2)]
+        for s in range(2):
+            nc.vector.quantize_mx(
+                out=table_codes[s][:].bitcast(FP8X4),
+                scales=table_scales[s][:],
+                in_=tables[s][:].rearrange("p j t -> p (j t)"),
+            )
+        second_mx = [quantize_values("second" + str(t), second_woven[t]) for t in range(PACK)]
+
+        result = sb.tile([P, PACK, N], F32, name="result")
+        out_rows = out_0.rearrange("(p t) j -> p t j", t=PACK)
+
+        def product(t, first_mx, cols, tag):
+            acc = banks.tile([P, cols.stop - cols.start], F32, name="acc", tag=tag)
+            for s, (codes, scales) in ((1, second_mx[t]), (0, first_mx)):
+                nc.tensor.matmul_mx(
+                    out=acc[:],
+                    lhsT=codes[:].bitcast(FP8X4),
+                    lhsT_scale=scales[:],
+                    rhs=table_codes[s][:, cols].bitcast(FP8X4),
+                    rhs_scale=table_scales[s][:, cols],
+                    start=(s == 1),
+                    stop=(s == 0),
+                )
+            nc.scalar.copy(result[:, t, cols], acc[:])
+            nc.sync.dma_start(out_rows[:, t, cols], result[:, t, cols])
+
+        last = PACK - 1
+        for t in range(PACK):
+            name = "first" + str(t)
+            listed = sb.tile([P, N], BF16, name=name + "_listed")
+            if t < last:
+                gather("scalar", listed[:], first_planes[t][:], token_list[:])
+            else:
+                gather("vector", listed[:, 0:HALF], first_planes[t][:], token_list[:, 0 : LIST_COLS // 2])
+                gather("scalar", listed[:, HALF:N], first_planes[t][:], token_list[:, LIST_COLS // 2 : LIST_COLS])
+            first_mx = quantize_values(name, turn_values(name, listed))
+            if t < last:
+                product(t, first_mx, slice(0, N), "bank" + str(t))
+            else:
+                product(t, first_mx, slice(0, HALF), "bank" + str(t))
+                product(t, first_mx, slice(HALF, N), "bank" + str(t + 1))
+
+        result_woven = [sb.tile([P, HALF, PACK], BF16, name="result_woven" + str(h), align_bytes=64) for h in range(2)]
+        nc.vector.tensor_copy(result_woven[0][:], result[:, :, 0:HALF].rearrange("p t j -> p j t"))
+        nc.vector.tensor_copy(
+            result_woven[1][:, 0:CHUNK, :], result[:, :, HALF : HALF + CHUNK].rearrange("p t j -> p j t")
+        )
+        nc.scalar.copy(result_woven[1][:, CHUNK:HALF, :], result[:, :, HALF + CHUNK : N].rearrange("p t j -> p j t"))
+        out_codes = sb.tile([P, N], U32, name="out_codes", align_bytes=64)
+        out_scales = sb.tile([P, N], U8, name="out_scales", align_bytes=64)
+        out_words = out_1[0].rearrange("p c r -> p (c r)").bitcast(I32)
+        for h in range(2):
+            cols = slice(h * HALF, (h + 1) * HALF)
+            nc.vector.quantize_mx(
+                out=out_codes[:, cols].bitcast(FP8X4),
+                scales=out_scales[:, cols],
+                in_=result_woven[h][:].rearrange("p j t -> p (j t)"),
+            )
+            nc.sync.dma_start(out_words[:, cols], out_codes[:, cols].bitcast(I32))
+        for q in range(4):
+            queue = nc.scalar if q < 2 else nc.sync
+            queue.dma_start(
+                out_2[0, 4 * q : 4 * q + 4, :].bitcast(I32), out_scales[32 * q : 32 * q + 4, :].bitcast(I32)
+            )

@@ -41,7 +41,7 @@ def tile_attend_tab_plain_twostores_pl_kernel(
             return tile
 
         def load_plane(name, src, t):
-            tile = sb.tile([P, src.shape[1]], F32, name=name + str(t))
+            tile = sb.tile([P, src.shape[1]], F32, name=name + str(t), align_bytes=64)
             nc.sync.dma_start(tile[:], src.rearrange("(p t) c -> p t c", t=PACK)[:, t, :])
             return tile
 
@@ -52,16 +52,7 @@ def tile_attend_tab_plain_twostores_pl_kernel(
                 nc.vector.tensor_copy(out, window.indirect(offsets))
 
         key_scale_pool = sb.tile([P, tokens], U8, name="key_scale_pool")
-        nc.gpsimd.memset(key_scale_pool[:].bitcast(I32), 0)
-        for q in range(4):
-            nc.gpsimd.dma_start(
-                key_scale_pool[32 * q : 32 * q + 4, :].bitcast(I32), keys_scales[0, 4 * q : 4 * q + 4, :].bitcast(I32)
-            )
-        factors = []
-        for name, src in (("factor1", rowf), ("factor2", rowf2)):
-            tile = sb.tile([P, PACK], F32, name=name)
-            nc.gpsimd.dma_start(tile[:], src.rearrange("(p t) o -> p (t o)", t=PACK))
-            factors.append(tile)
+        nc.vector.memset(key_scale_pool[:].bitcast(I32), 0)
         ident = sb.tile([P, P], F32, name="ident")
         make_identity(nc, ident[:])
 
@@ -69,69 +60,85 @@ def tile_attend_tab_plain_twostores_pl_kernel(
         key_word_pool = sb.tile([P, tokens], U16, name="key_word_pool")
         nc.sync.dma_start(key_word_pool[:].bitcast(I32), keys_words[0].bitcast(I32))
         note_list = load_list("note_list", offs2)
+        for q in range(4):
+            nc.sync.dma_start(
+                key_scale_pool[32 * q : 32 * q + 4, :].bitcast(I32), keys_scales[0, 4 * q : 4 * q + 4, :].bitcast(I32)
+            )
         note_planes = [load_plane("notes", notes, t) for t in range(PACK)]
         second_list = load_list("second_list", offs3)
-        second_planes = [load_plane("second", vals2, t) for t in range(PACK)]
+        second_planes = [load_plane("second", vals2, t) for t in range(2)]
+        factors = []
+        for name, src in (("factor1", rowf), ("factor2", rowf2)):
+            tile = sb.tile([P, PACK], F32, name=name)
+            nc.sync.dma_start(tile[:], src.rearrange("(p t) o -> p (t o)", t=PACK))
+            factors.append(tile)
+        second_planes.extend([load_plane("second", vals2, t) for t in range(2, PACK)])
         first_planes = [load_plane("first", vals, t) for t in range(PACK)]
 
         key_words_listed = sb.tile([P, N], U16, name="key_words_listed")
         nc.vector.tensor_copy(key_words_listed[:], key_word_pool[:].indirect(token_list[:]))
+        key_scales = sb.tile([P, PACK, P], U8, name="key_scales", align_bytes=64)
+        nc.vector.tensor_copy(key_scales[:].rearrange("p t m -> p m t"), key_scale_pool[:].indirect(token_list[:]))
         key_words = sb.tile([P, PACK, P], U16, name="key_words", align_bytes=64)
         nc.vector.tensor_copy(key_words[:], key_words_listed[:].rearrange("p (m t) -> p t m", t=PACK))
 
-        notes_listed = sb.tile([P, PACK, N], BF16, name="notes_listed")
+        notes_row = sb.tile([P, PACK * N], BF16, name="notes_row")
+        notes_listed = notes_row[:].rearrange("p (t j) -> p t j", t=PACK)
         gather("scalar", notes_listed[:, 0, :], note_planes[0][:], note_list[:])
         gather("vector", notes_listed[:, 1, :], note_planes[1][:], note_list[:])
         gather("scalar", notes_listed[:, 2, :], note_planes[2][:], note_list[:])
-
-        key_scales = sb.tile([P, PACK, P], U8, name="key_scales", align_bytes=64)
-        nc.vector.tensor_copy(key_scales[:].rearrange("p t m -> p m t"), key_scale_pool[:].indirect(token_list[:]))
-
         gather("vector", notes_listed[:, 3, 0:HALF], note_planes[3][:], note_list[:, 0 : LIST_COLS // 2])
         gather("scalar", notes_listed[:, 3, HALF:N], note_planes[3][:], note_list[:, LIST_COLS // 2 : LIST_COLS])
 
         note_codes = sb.tile([P, N], U32, name="note_codes", align_bytes=64)
         note_scales = sb.tile([P, N], U8, name="note_scales", align_bytes=64)
-        notes_woven = [sb.tile([P, HALF, PACK], BF16, name="notes_woven" + str(h), align_bytes=64) for h in range(2)]
-        for h in range(2):
-            cols = slice(h * HALF, (h + 1) * HALF)
-            nc.vector.tensor_copy(notes_woven[h][:], notes_listed[:, :, cols].rearrange("p t j -> p j t"))
-        for h in range(2):
-            cols = slice(h * HALF, (h + 1) * HALF)
-            nc.vector.quantize_mx(
-                out=note_codes[:, cols].bitcast(FP8X4),
-                scales=note_scales[:, cols],
-                in_=notes_woven[h][:].rearrange("p j t -> p (j t)"),
+        notes_woven = [sb.tile([P, CHUNK, PACK], BF16, name="notes_woven" + str(c), align_bytes=64) for c in range(PACK)]
+        for c in range(PACK + 1):
+            if c < PACK:
+                cols = slice(c * CHUNK, (c + 1) * CHUNK)
+                nc.vector.tensor_copy(notes_woven[c][:], notes_listed[:, :, cols].rearrange("p t j -> p j t"))
+            if c > 0:
+                cols = slice((c - 1) * CHUNK, c * CHUNK)
+                nc.vector.quantize_mx(
+                    out=note_codes[:, cols].bitcast(FP8X4),
+                    scales=note_scales[:, cols],
+                    in_=notes_woven[c - 1][:].rearrange("p j t -> p (j t)"),
+                )
+
+        def list_values(name, planes, offsets, t):
+            listed = sb.tile([P, N], BF16, name=name + "_listed" + str(t), align_bytes=64)
+            if planes is first_planes and t == PACK - 1:
+                gather("vector", listed[:, 0:HALF], planes[t][:], offsets[:, 0 : LIST_COLS // 2])
+                gather("scalar", listed[:, HALF:N], planes[t][:], offsets[:, LIST_COLS // 2 : LIST_COLS])
+            else:
+                gather("scalar", listed[:], planes[t][:], offsets[:])
+            return listed
+
+        def turn_values(listed_planes):
+            turned = turn.tile([P, len(listed_planes), 2, P], F32, name="turned")
+            for k, listed in enumerate(listed_planes):
+                words = listed[:].bitcast(F32)
+                for u in range(2):
+                    nc.tensor.transpose(turned[:, k, u, :], words[:, u : 2 * P : 2], ident[:])
+            return turned
+
+        def weave_values(woven, turned):
+            nc.scalar.copy(
+                woven.bitcast(F32).rearrange("p (k m u) -> p k m u", m=P, u=2), turned[:].rearrange("p k u m -> p k m u")
             )
 
-        def turn_values(name, listed):
-            words = listed[:].bitcast(F32)
-            turned = turn.tile([P, 2, P], F32, name="turned")
-            for u in range(2):
-                nc.tensor.transpose(turned[:, u, :], words[:, u : 2 * P : 2], ident[:])
-            woven = sb.tile([P, P * PACK], BF16, name=name + "_woven", align_bytes=64)
-            nc.scalar.copy(woven[:].bitcast(F32).rearrange("p (m u) -> p m u", u=2), turned[:].rearrange("p u m -> p m u"))
-            return woven
-
-        def quantize_values(name, woven):
-            codes = sb.tile([P, P], U32, name=name + "_codes", align_bytes=64)
-            scales = sb.tile([P, P], U8, name=name + "_scales", align_bytes=64)
-            nc.vector.quantize_mx(out=codes[:].bitcast(FP8X4), scales=scales[:], in_=woven[:])
+        def quantize(name, woven, slot=""):
+            width = woven.shape[1] // PACK
+            codes = sb.tile([P, width], U32, name=name + "_codes", tag=slot, align_bytes=64)
+            scales = sb.tile([P, width], U8, name=name + "_scales", align_bytes=64)
+            nc.vector.quantize_mx(out=codes[:].bitcast(FP8X4), scales=scales[:], in_=woven)
             return codes, scales
 
-        second_woven = []
-
-        def second_plane(t):
-            listed = sb.tile([P, N], BF16, name="second_listed" + str(t))
-            gather("scalar", listed[:], second_planes[t][:], second_list[:])
-            second_woven.append(turn_values("second" + str(t), listed))
-
-        second_plane(0)
-
-        tables = [sb.tile([P, N, PACK], BF16, name="table" + str(s), align_bytes=64) for s in range(2)]
+        raws = []
         for c in range(PACK):
             cols = slice(c * CHUNK, (c + 1) * CHUNK)
             raw = banks.tile([P, PACK, CHUNK], F32, name="raw", tag="bank" + str(c))
+            raws.append(raw)
             for t in range(PACK):
                 nc.tensor.matmul_mx(
                     out=raw[:, t, :],
@@ -142,61 +149,101 @@ def tile_attend_tab_plain_twostores_pl_kernel(
                     start=True,
                     stop=True,
                 )
-            for s in range(2):
+
+        def scaled_table(name, factor):
+            table = sb.tile([P, N * PACK], BF16, name=name, align_bytes=64)
+            for c in range(PACK):
                 nc.vector.scalar_tensor_tensor(
-                    out=tables[s][:, cols, :],
-                    in0=raw[:].rearrange("p t j -> p j t"),
+                    out=table[:, c * N : (c + 1) * N].rearrange("p (j t) -> p j t", t=PACK),
+                    in0=raws[c][:].rearrange("p t j -> p j t"),
                     scalar=0.0,
-                    in1=factors[s][:].unsqueeze(1).broadcast_to([P, CHUNK, PACK]),
+                    in1=factor[:].unsqueeze(1).broadcast_to([P, CHUNK, PACK]),
                     op0=ALU.max,
                     op1=ALU.mult,
                 )
-            if c + 1 < PACK:
-                second_plane(c + 1)
+            return table[:]
 
-        table_codes = [sb.tile([P, N], U32, name="table_codes" + str(s), align_bytes=64) for s in range(2)]
-        table_scales = [sb.tile([P, N], U8, name="table_scales" + str(s), align_bytes=64) for s in range(2)]
-        for s in range(2):
-            nc.vector.quantize_mx(
-                out=table_codes[s][:].bitcast(FP8X4),
-                scales=table_scales[s][:],
-                in_=tables[s][:].rearrange("p j t -> p (j t)"),
-            )
-        second_mx = [quantize_values("second" + str(t), second_woven[t]) for t in range(PACK)]
+        second_listed = [list_values("second", second_planes, second_list, t) for t in range(PACK)]
+        second_turned = [turn_values(second_listed[2 * k : 2 * k + 2]) for k in range(2)]
+        first_listed = []
 
-        result = sb.tile([P, PACK, N], F32, name="result")
+        def list_first(t):
+            first_listed.append(list_values("first", first_planes, token_list, t))
+
+        table2 = scaled_table("table2", factors[1])
+        second_woven = sb.tile([P, PACK * N], BF16, name="second_woven", tag="second3", align_bytes=64)
+        for k in range(2):
+            weave_values(second_woven[:, 2 * k * N : 2 * (k + 1) * N], second_turned[k])
+        list_first(0)
+        table1 = scaled_table("table1", factors[0])
+        table2_mx = quantize("table2", table2)
+        table1_mx = quantize("table1", table1)
+
         out_rows = out_0.rearrange("(p t) j -> p t j", t=PACK)
+        last = PACK - 1
+        parts = [(t, slice(0, N)) for t in range(last)] + [(last, slice(0, HALF)), (last, slice(HALF, N))]
+        sums = []
 
-        def product(t, first_mx, cols, tag):
-            acc = banks.tile([P, cols.stop - cols.start], F32, name="acc", tag=tag)
-            for s, (codes, scales) in ((1, second_mx[t]), (0, first_mx)):
-                nc.tensor.matmul_mx(
-                    out=acc[:],
-                    lhsT=codes[:].bitcast(FP8X4),
-                    lhsT_scale=scales[:],
-                    rhs=table_codes[s][:, cols].bitcast(FP8X4),
-                    rhs_scale=table_scales[s][:, cols],
-                    start=(s == 1),
-                    stop=(s == 0),
-                )
-            nc.scalar.copy(result[:, t, cols], acc[:])
+        def product(acc, values_mx, rows, table_mx, cols, opens):
+            nc.tensor.matmul_mx(
+                out=acc[:],
+                lhsT=values_mx[0][:, rows].bitcast(FP8X4),
+                lhsT_scale=values_mx[1][:, rows],
+                rhs=table_mx[0][:, cols].bitcast(FP8X4),
+                rhs_scale=table_mx[1][:, cols],
+                start=opens,
+                stop=not opens,
+            )
+
+        def open_second(pair):
+            values_mx = quantize(
+                "second" + str(pair), second_woven[:, 2 * pair * N : 2 * (pair + 1) * N], "first_listed" + str(pair)
+            )
+            for k, (t, cols) in enumerate(parts):
+                if t // 2 == pair:
+                    acc = banks.tile([P, cols.stop - cols.start], F32, name="acc", tag="bank" + str(k))
+                    sums.append(acc)
+                    product(acc, values_mx, slice(t % 2 * P, (t % 2 + 1) * P), table2_mx, cols, True)
+
+        def close_first(name, woven, planes):
+            values_mx = quantize(name, woven)
+            for k, (t, cols) in enumerate(parts):
+                if t in planes:
+                    rows = slice((t - planes[0]) * P, (t - planes[0] + 1) * P)
+                    product(sums[k], values_mx, rows, table1_mx, cols, False)
+
+        def store(k, engine):
+            t, cols = parts[k]
+            if engine == "scalar":
+                nc.scalar.copy(result[:, t, cols], sums[k][:])
+            else:
+                nc.vector.tensor_copy(result[:, t, cols], sums[k][:])
             nc.sync.dma_start(out_rows[:, t, cols], result[:, t, cols])
 
-        last = PACK - 1
-        for t in range(PACK):
-            name = "first" + str(t)
-            listed = sb.tile([P, N], BF16, name=name + "_listed")
-            if t < last:
-                gather("scalar", listed[:], first_planes[t][:], token_list[:])
-            else:
-                gather("vector", listed[:, 0:HALF], first_planes[t][:], token_list[:, 0 : LIST_COLS // 2])
-                gather("scalar", listed[:, HALF:N], first_planes[t][:], token_list[:, LIST_COLS // 2 : LIST_COLS])
-            first_mx = quantize_values(name, turn_values(name, listed))
-            if t < last:
-                product(t, first_mx, slice(0, N), "bank" + str(t))
-            else:
-                product(t, first_mx, slice(0, HALF), "bank" + str(t))
-                product(t, first_mx, slice(HALF, N), "bank" + str(t + 1))
+        list_first(1)
+        early_turned = turn_values(first_listed[0:2])
+        open_second(0)
+        open_second(1)
+        list_first(2)
+        third_turned = turn_values(first_listed[2:3])
+        early_woven = sb.tile([P, 2 * N], BF16, name="early_woven", tag="first2", align_bytes=64)
+        weave_values(early_woven[:], early_turned)
+        close_first("early", early_woven[:], (0, 1))
+        list_first(3)
+        last_turned = turn_values(first_listed[3:4])
+        late = sb.tile([P, PACK * N + HALF], F32, name="late", tag="first3", align_bytes=64)
+        result = late[:, 0 : PACK * N].rearrange("p (t j) -> p t j", t=PACK)
+        third_woven = late[:, PACK * N : PACK * N + HALF].bitcast(BF16)
+        weave_values(third_woven, third_turned)
+        store(0, "vector")
+        close_first("third", third_woven, (2,))
+        last_woven = sb.tile([P, N], BF16, name="last_woven", align_bytes=64)
+        weave_values(last_woven[:], last_turned)
+        close_first("last", last_woven[:], (3,))
+        store(1, "scalar")
+        store(2, "vector")
+        store(3, "scalar")
+        store(4, "scalar")
 
         result_woven = [sb.tile([P, HALF, PACK], BF16, name="result_woven" + str(h), align_bytes=64) for h in range(2)]
         nc.vector.tensor_copy(result_woven[0][:], result[:, :, 0:HALF].rearrange("p t j -> p j t"))

@@ -51,6 +51,9 @@ def tile_attend_tab_plain_twostores_pl_kernel(
             else:
                 nc.vector.tensor_copy(out, window.indirect(offsets))
 
+        def interleave(copy, woven, planes):
+            copy(woven.rearrange("p (c i) t -> p c t i", i=PACK), planes.rearrange("p t (c i) -> p c t i", i=PACK))
+
         key_scale_pool = sb.tile([P, tokens], U8, name="key_scale_pool")
         nc.vector.memset(key_scale_pool[:].bitcast(I32), 0)
         ident = sb.tile([P, P], F32, name="ident")
@@ -77,10 +80,12 @@ def tile_attend_tab_plain_twostores_pl_kernel(
 
         key_words_listed = sb.tile([P, N], U16, name="key_words_listed")
         nc.vector.tensor_copy(key_words_listed[:], key_word_pool[:].indirect(token_list[:]))
-        key_scales = sb.tile([P, PACK, P], U8, name="key_scales", align_bytes=64)
-        nc.vector.tensor_copy(key_scales[:].rearrange("p t m -> p m t"), key_scale_pool[:].indirect(token_list[:]))
+        key_scales_listed = sb.tile([P, N], U8, name="key_scales_listed")
+        nc.vector.tensor_copy(key_scales_listed[:], key_scale_pool[:].indirect(token_list[:]))
         key_words = sb.tile([P, PACK, P], U16, name="key_words", align_bytes=64)
         nc.vector.tensor_copy(key_words[:], key_words_listed[:].rearrange("p (m t) -> p t m", t=PACK))
+        key_scales = sb.tile([P, PACK, P], U8, name="key_scales", align_bytes=64)
+        nc.vector.tensor_copy(key_scales[:], key_scales_listed[:].rearrange("p (m t) -> p t m", t=PACK))
 
         notes_row = sb.tile([P, PACK * N], BF16, name="notes_row")
         notes_listed = notes_row[:].rearrange("p (t j) -> p t j", t=PACK)
@@ -96,7 +101,7 @@ def tile_attend_tab_plain_twostores_pl_kernel(
         for c in range(PACK + 1):
             if c < PACK:
                 cols = slice(c * CHUNK, (c + 1) * CHUNK)
-                nc.vector.tensor_copy(notes_woven[c][:], notes_listed[:, :, cols].rearrange("p t j -> p j t"))
+                interleave(nc.vector.tensor_copy, notes_woven[c][:], notes_listed[:, :, cols])
             if c > 0:
                 cols = slice((c - 1) * CHUNK, c * CHUNK)
                 nc.vector.quantize_mx(
@@ -212,13 +217,12 @@ def tile_attend_tab_plain_twostores_pl_kernel(
                     rows = slice((t - planes[0]) * P, (t - planes[0] + 1) * P)
                     product(sums[k], values_mx, rows, table1_mx, cols, False)
 
-        def store(k, engine):
+        def empty(k, copy):
             t, cols = parts[k]
-            if engine == "scalar":
-                nc.scalar.copy(result[:, t, cols], sums[k][:])
-            else:
-                nc.vector.tensor_copy(result[:, t, cols], sums[k][:])
-            nc.sync.dma_start(out_rows[:, t, cols], result[:, t, cols])
+            copy(result[:, t, cols], sums[k][:])
+
+        def store(planes):
+            nc.sync.dma_start(out_rows[:, planes, :], result[:, planes, :])
 
         list_first(1)
         early_turned = turn_values(first_listed[0:2])
@@ -235,22 +239,23 @@ def tile_attend_tab_plain_twostores_pl_kernel(
         result = late[:, 0 : PACK * N].rearrange("p (t j) -> p t j", t=PACK)
         third_woven = late[:, PACK * N : PACK * N + HALF].bitcast(BF16)
         weave_values(third_woven, third_turned)
-        store(0, "vector")
+        empty(0, nc.vector.tensor_copy)
         close_first("third", third_woven, (2,))
         last_woven = sb.tile([P, N], BF16, name="last_woven", align_bytes=64)
         weave_values(last_woven[:], last_turned)
         close_first("last", last_woven[:], (3,))
-        store(1, "scalar")
-        store(2, "vector")
-        store(3, "scalar")
-        store(4, "scalar")
+        empty(1, nc.vector.tensor_copy)
+        store(slice(0, 2))
+        empty(2, nc.scalar.copy)
+        store(slice(2, 3))
+        empty(3, nc.scalar.copy)
+        empty(4, nc.scalar.copy)
+        store(slice(3, 4))
 
         result_woven = [sb.tile([P, HALF, PACK], BF16, name="result_woven" + str(h), align_bytes=64) for h in range(2)]
-        nc.vector.tensor_copy(result_woven[0][:], result[:, :, 0:HALF].rearrange("p t j -> p j t"))
-        nc.vector.tensor_copy(
-            result_woven[1][:, 0:CHUNK, :], result[:, :, HALF : HALF + CHUNK].rearrange("p t j -> p j t")
-        )
-        nc.scalar.copy(result_woven[1][:, CHUNK:HALF, :], result[:, :, HALF + CHUNK : N].rearrange("p t j -> p j t"))
+        interleave(nc.vector.tensor_copy, result_woven[0][:], result[:, :, 0:HALF])
+        interleave(nc.vector.tensor_copy, result_woven[1][:, 0:CHUNK, :], result[:, :, HALF : HALF + CHUNK])
+        interleave(nc.scalar.copy, result_woven[1][:, CHUNK:HALF, :], result[:, :, HALF + CHUNK : N])
         out_codes = sb.tile([P, N], U32, name="out_codes", align_bytes=64)
         out_scales = sb.tile([P, N], U8, name="out_scales", align_bytes=64)
         out_words = out_1[0].rearrange("p c r -> p (c r)").bitcast(I32)

from contextlib import ExitStack

import concourse.mybir as mybir
from concourse.masks import make_identity

FLOPS = 2 * 512 * 512 * 512 * 3

F32 = mybir.dt.float32
BF16 = mybir.dt.bfloat16
I32 = mybir.dt.int32
U32 = mybir.dt.uint32
U16 = mybir.dt.uint16
U8 = mybir.dt.uint8
FP8X4 = mybir.dt.float8_e4m3fn_x4
FP4X4 = mybir.dt.float4_e2m1fn_x4
COPY = mybir.ActivationFunctionType.Copy
ALU = mybir.AluOpType

P = 128
PACK = 4
N = 512
HALF = N // 2
CHUNK = N // PACK
LIST_COLS = N // 16


def tile_attend_tab_plain_twostores_pl_kernel(
    tc, keys_words, keys_scales, notes, rowf, rowf2, vals, vals2, offs, offs2, offs3, out_0, out_1, out_2
):
    nc = tc.nc
    tokens = vals.shape[1]

    with ExitStack() as ctx:
        sb = ctx.enter_context(tc.tile_pool(name="sb", bufs=1))
        banks = ctx.enter_context(tc.psum_pool(name="banks", bufs=1))
        turn = ctx.enter_context(tc.psum_pool(name="turn", bufs=3))

        def load_list(name, src):
            tile = sb.tile([P, LIST_COLS], U16, name=name)
            nc.sync.dma_start(tile[:], src)
            return tile

        def load_plane(name, src, t):
            tile = sb.tile([P, src.shape[1]], F32, name=name + str(t), align_bytes=64)
            nc.sync.dma_start(tile[:], src.rearrange("(p t) c -> p t c", t=PACK)[:, t, :])
            return tile

        def gather(engine, out, window, offsets):
            if engine == "scalar":
                nc.scalar.activation(out, window.indirect(offsets), COPY)
            else:
                nc.vector.tensor_copy(out, window.indirect(offsets))

        def interleave(copy, woven, planes):
            copy(woven.rearrange("p (c i) t -> p c t i", i=PACK), planes.rearrange("p t (c i) -> p c t i", i=PACK))

        key_scale_pool = sb.tile([P, tokens], U8, name="key_scale_pool")
        nc.vector.memset(key_scale_pool[:].bitcast(I32), 0)
        ident = sb.tile([P, P], F32, name="ident")
        make_identity(nc, ident[:])

        token_list = load_list("token_list", offs)
        key_word_pool = sb.tile([P, tokens], U16, name="key_word_pool")
        nc.sync.dma_start(key_word_pool[:].bitcast(I32), keys_words[0].bitcast(I32))
        note_list = load_list("note_list", offs2)
        for q in range(4):
            nc.sync.dma_start(
                key_scale_pool[32 * q : 32 * q + 4, :].bitcast(I32), keys_scales[0, 4 * q : 4 * q + 4, :].bitcast(I32)
            )
        note_planes = [load_plane("notes", notes, t) for t in range(PACK)]
        second_list = load_list("second_list", offs3)
        second_planes = [load_plane("second", vals2, t) for t in range(2)]
        factors = []
        for name, src in (("factor1", rowf), ("factor2", rowf2)):
            tile = sb.tile([P, PACK], F32, name=name)
            nc.sync.dma_start(tile[:], src.rearrange("(p t) o -> p (t o)", t=PACK))
            factors.append(tile)
        second_planes.extend([load_plane("second", vals2, t) for t in range(2, PACK)])
        first_planes = [load_plane("first", vals, t) for t in range(PACK)]

        key_words_listed = sb.tile([P, N], U16, name="key_words_listed")
        nc.vector.tensor_copy(key_words_listed[:], key_word_pool[:].indirect(token_list[:]))
        key_scales_listed = sb.tile([P, N], U8, name="key_scales_listed")
        nc.vector.tensor_copy(key_scales_listed[:], key_scale_pool[:].indirect(token_list[:]))
        key_words = sb.tile([P, PACK, P], U16, name="key_words", align_bytes=64)
        nc.vector.tensor_copy(key_words[:], key_words_listed[:].rearrange("p (m t) -> p t m", t=PACK))
        key_scales = sb.tile([P, PACK, P], U8, name="key_scales", align_bytes=64)
        nc.vector.tensor_copy(key_scales[:], key_scales_listed[:].rearrange("p (m t) -> p t m", t=PACK))

        notes_row = sb.tile([P, PACK * N], BF16, name="notes_row")
        notes_listed = notes_row[:].rearrange("p (t j) -> p t j", t=PACK)
        gather("scalar", notes_listed[:, 0, :], note_planes[0][:], note_list[:])
        gather("vector", notes_listed[:, 1, :], note_planes[1][:], note_list[:])
        gather("scalar", notes_listed[:, 2, :], note_planes[2][:], note_list[:])
        gather("vector", notes_listed[:, 3, 0:HALF], note_planes[3][:], note_list[:, 0 : LIST_COLS // 2])
        gather("scalar", notes_listed[:, 3, HALF:N], note_planes[3][:], note_list[:, LIST_COLS // 2 : LIST_COLS])

        note_codes = sb.tile([P, N], U32, name="note_codes", align_bytes=64)
        note_scales = sb.tile([P, N], U8, name="note_scales", align_bytes=64)
        notes_woven = [sb.tile([P, CHUNK, PACK], BF16, name="notes_woven" + str(c), align_bytes=64) for c in range(PACK)]
        for c in range(PACK + 1):
            if c < PACK:
                cols = slice(c * CHUNK, (c + 1) * CHUNK)
                interleave(nc.vector.tensor_copy, notes_woven[c][:], notes_listed[:, :, cols])
            if c > 0:
                cols = slice((c - 1) * CHUNK, c * CHUNK)
                nc.vector.quantize_mx(
                    out=note_codes[:, cols].bitcast(FP8X4),
                    scales=note_scales[:, cols],
                    in_=notes_woven[c - 1][:].rearrange("p j t -> p (j t)"),
                )

        def list_values(name, planes, offsets, t):
            listed = sb.tile([P, N], BF16, name=name + "_listed" + str(t), align_bytes=64)
            if planes is first_planes and t == PACK - 1:
                gather("vector", listed[:, 0:HALF], planes[t][:], offsets[:, 0 : LIST_COLS // 2])
                gather("scalar", listed[:, HALF:N], planes[t][:], offsets[:, LIST_COLS // 2 : LIST_COLS])
            else:
                gather("scalar", listed[:], planes[t][:], offsets[:])
            return listed

        def turn_values(listed_planes):
            turned = turn.tile([P, len(listed_planes), 2, P], F32, name="turned")
            for k, listed in enumerate(listed_planes):
                words = listed[:].bitcast(F32)
                for u in range(2):
                    nc.tensor.transpose(turned[:, k, u, :], words[:, u : 2 * P : 2], ident[:])
            return turned

        def weave_values(woven, turned):
            nc.scalar.copy(
                woven.bitcast(F32).rearrange("p (k m u) -> p k m u", m=P, u=2), turned[:].rearrange("p k u m -> p k m u")
            )

        def quantize(name, woven, slot=""):
            width = woven.shape[1] // PACK
            codes = sb.tile([P, width], U32, name=name + "_codes", tag=slot, align_bytes=64)
            scales = sb.tile([P, width], U8, name=name + "_scales", align_bytes=64)
            nc.vector.quantize_mx(out=codes[:].bitcast(FP8X4), scales=scales[:], in_=woven)
            return codes, scales

        raws = []
        for c in range(PACK):
            cols = slice(c * CHUNK, (c + 1) * CHUNK)
            raw = banks.tile([P, PACK, CHUNK], F32, name="raw", tag="bank" + str(c))
            raws.append(raw)
            for t in range(PACK):
                nc.tensor.matmul_mx(
                    out=raw[:, t, :],
                    lhsT=key_words[:, t, :].bitcast(FP4X4),
                    lhsT_scale=key_scales[:, t, :],
                    rhs=note_codes[:, cols].bitcast(FP8X4),
                    rhs_scale=note_scales[:, cols],
                    start=True,
                    stop=True,
                )

        def scaled_table(name, factor):
            table = sb.tile([P, N * PACK], BF16, name=name, align_bytes=64)
            for c in range(PACK):
                nc.vector.scalar_tensor_tensor(
                    out=table[:, c * N : (c + 1) * N].rearrange("p (j t) -> p j t", t=PACK),
                    in0=raws[c][:].rearrange("p t j -> p j t"),
                    scalar=0.0,
                    in1=factor[:].unsqueeze(1).broadcast_to([P, CHUNK, PACK]),
                    op0=ALU.max,
                    op1=ALU.mult,
                )
            return table[:]

        second_listed = [list_values("second", second_planes, second_list, t) for t in range(PACK)]
        second_turned = [turn_values(second_listed[2 * k : 2 * k + 2]) for k in range(2)]
        first_listed = []

        def list_first(t):
            first_listed.append(list_values("first", first_planes, token_list, t))

        table2 = scaled_table("table2", factors[1])
        second_woven = sb.tile([P, PACK * N], BF16, name="second_woven", tag="second3", align_bytes=64)
        for k in range(2):
            weave_values(second_woven[:, 2 * k * N : 2 * (k + 1) * N], second_turned[k])
        list_first(0)
        table1 = scaled_table("table1", factors[0])
        table2_mx = quantize("table2", table2)
        table1_mx = quantize("table1", table1)

        out_rows = out_0.rearrange("(p t) j -> p t j", t=PACK)
        last = PACK - 1
        parts = [(t, slice(0, N)) for t in range(last)] + [(last, slice(0, HALF)), (last, slice(HALF, N))]
        sums = []

        def product(acc, values_mx, rows, table_mx, cols, opens):
            nc.tensor.matmul_mx(
                out=acc[:],
                lhsT=values_mx[0][:, rows].bitcast(FP8X4),
                lhsT_scale=values_mx[1][:, rows],
                rhs=table_mx[0][:, cols].bitcast(FP8X4),
                rhs_scale=table_mx[1][:, cols],
                start=opens,
                stop=not opens,
            )

        def open_second(pair):
            values_mx = quantize(
                "second" + str(pair), second_woven[:, 2 * pair * N : 2 * (pair + 1) * N], "first_listed" + str(pair)
            )
            for k, (t, cols) in enumerate(parts):
                if t // 2 == pair:
                    acc = banks.tile([P, cols.stop - cols.start], F32, name="acc", tag="bank" + str(k))
                    sums.append(acc)
                    product(acc, values_mx, slice(t % 2 * P, (t % 2 + 1) * P), table2_mx, cols, True)

        def close_first(name, woven, planes):
            values_mx = quantize(name, woven)
            for k, (t, cols) in enumerate(parts):
                if t in planes:
                    rows = slice((t - planes[0]) * P, (t - planes[0] + 1) * P)
                    product(sums[k], values_mx, rows, table1_mx, cols, False)

        def empty(k, copy):
            t, cols = parts[k]
            copy(result[:, t, cols], sums[k][:])

        def store(planes):
            nc.sync.dma_start(out_rows[:, planes, :], result[:, planes, :])

        list_first(1)
        early_turned = turn_values(first_listed[0:2])
        open_second(0)
        open_second(1)
        list_first(2)
        third_turned = turn_values(first_listed[2:3])
        early_woven = sb.tile([P, 2 * N], BF16, name="early_woven", tag="first2", align_bytes=64)
        weave_values(early_woven[:], early_turned)
        close_first("early", early_woven[:], (0, 1))
        list_first(3)
        last_turned = turn_values(first_listed[3:4])
        late = sb.tile([P, PACK * N + HALF], F32, name="late", tag="first3", align_bytes=64)
        result = late[:, 0 : PACK * N].rearrange("p (t j) -> p t j", t=PACK)
        third_woven = late[:, PACK * N : PACK * N + HALF].bitcast(BF16)
        weave_values(third_woven, third_turned)
        empty(0, nc.vector.tensor_copy)
        close_first("third", third_woven, (2,))
        last_woven = sb.tile([P, N], BF16, name="last_woven", align_bytes=64)
        weave_values(last_woven[:], last_turned)
        close_first("last", last_woven[:], (3,))
        empty(1, nc.vector.tensor_copy)
        store(slice(0, 2))
        empty(2, nc.scalar.copy)
        store(slice(2, 3))
        empty(3, nc.scalar.copy)
        empty(4, nc.scalar.copy)
        store(slice(3, 4))

        result_woven = [sb.tile([P, HALF, PACK], BF16, name="result_woven" + str(h), align_bytes=64) for h in range(2)]
        interleave(nc.vector.tensor_copy, result_woven[0][:], result[:, :, 0:HALF])
        interleave(nc.vector.tensor_copy, result_woven[1][:, 0:CHUNK, :], result[:, :, HALF : HALF + CHUNK])
        interleave(nc.scalar.copy, result_woven[1][:, CHUNK:HALF, :], result[:, :, HALF + CHUNK : N])
        out_codes = sb.tile([P, N], U32, name="out_codes", align_bytes=64)
        out_scales = sb.tile([P, N], U8, name="out_scales", align_bytes=64)
        out_words = out_1[0].rearrange("p c r -> p (c r)").bitcast(I32)
        for h in range(2):
            cols = slice(h * HALF, (h + 1) * HALF)
            nc.vector.quantize_mx(
                out=out_codes[:, cols].bitcast(FP8X4),
                scales=out_scales[:, cols],
                in_=result_woven[h][:].rearrange("p j t -> p (j t)"),
            )
            nc.sync.dma_start(out_words[:, cols], out_codes[:, cols].bitcast(I32))
        for q in range(4):
            queue = nc.scalar if q < 2 else nc.sync
            queue.dma_start(
                out_2[0, 4 * q : 4 * q + 4, :].bitcast(I32), out_scales[32 * q : 32 * q + 4, :].bitcast(I32)
            )
